import numpy as np
import ml_dtypes


def mxq(x, axis, fmt="e4m3"):
    dtype, down = {"e4m3": (ml_dtypes.float8_e4m3fn, 7), "e5m2": (ml_dtypes.float8_e5m2, 14)}[fmt]
    v = np.moveaxis(np.asarray(x, np.float32).astype(ml_dtypes.bfloat16).astype(np.float64), axis, -1)
    blocks = v.reshape(v.shape[:-1] + (-1, 32))
    amax = np.abs(blocks).max(-1, keepdims=True)
    byte = np.maximum(np.where(amax > 0, np.frexp(amax)[1] - 1 + 127, 0) - down, 1)
    scale = np.exp2(byte - 127.0)
    codes = (blocks / scale).astype(np.float32).astype(dtype).astype(np.float64)
    return np.moveaxis((codes * scale).reshape(v.shape), -1, axis)


WIDE = False


def mx_kscale(k):
    if not WIDE:
        return np.ones(k)
    levels = np.array([10, -10, 5, -5, 0])
    if k % 512:
        return np.exp2(np.random.permutation(np.resize(levels, k // 32))).repeat(32)
    a = np.empty((k // 512, 16))
    for p in range(k // 512):
        a[p, :8] = np.random.permutation(np.resize(levels, 8))
        for g in range(8):
            far = levels[np.abs(levels - a[p, g]) >= 10]
            a[p, g + 8] = far[np.random.randint(len(far))]
    return np.exp2(a.ravel()).repeat(32)


def f64(x):
    return np.asarray(x).astype(np.float64)


def striped(idx):
    return np.tile(idx.reshape(-1, 16).T, (8, 1)).astype(np.uint16)


def unstriped(offs):
    return offs[:16].T.reshape(-1).astype(np.int64)


def striped8(idx):
    return np.concatenate([x.reshape(-1, 16).T for x in idx]).astype(np.uint16)


def runs(offs, k):
    lists = np.stack([offs[16 * r : 16 * r + 16].T.reshape(-1) for r in range(8)]).astype(np.int64)
    return lists[np.arange(k) % 512 // 64]


def pack_weight(w):
    k, n = w.shape
    w = f64(np.asarray(w, np.float32).astype(ml_dtypes.bfloat16)).reshape(k // 32, 32, n)
    amax = np.abs(w).max(1)
    byte = np.clip(np.where(amax > 0, np.frexp(amax)[1] - 1 + 127 - 7, 1), 1, 254)
    scaled = (w * np.exp2(127.0 - byte)[:, None, :]).reshape(k, n).astype(np.float32)
    words = np.ascontiguousarray(scaled.reshape(k // 512, 128, 4, n).transpose(0, 1, 3, 2)).astype(ml_dtypes.float8_e4m3fn).view(np.uint8)
    return words, np.ascontiguousarray(byte.astype(np.uint8).reshape(k // 512, 16, n))


def unpack_weight(words, scales):
    g, p, n, _ = words.shape
    vals = np.ascontiguousarray(words).view(ml_dtypes.float8_e4m3fn).astype(np.float64) * np.repeat(np.exp2(scales.astype(np.float64) - 127.0), 8, axis=1)[..., None]
    return vals.transpose(0, 1, 3, 2).reshape(g * 512, n)


def relu(v):
    return np.maximum(v, 0.0)

def planes(y):
    n, m = y.shape
    v = y.astype(np.float32).astype(ml_dtypes.bfloat16).astype(np.float64).reshape(n // 32, 32, m)
    top = np.abs(v).max(1)
    byte = np.clip(np.where(top > 0, np.frexp(top)[1] - 1 + 127 - 7, 1), 1, 254)
    codes = (v * np.exp2(127.0 - byte)[:, None, :]).reshape(n, m).astype(np.float32).astype(ml_dtypes.float8_e4m3fn).view(np.uint8)
    words = codes.reshape(n // 512, 128, 4, m).transpose(0, 1, 3, 2)
    return np.ascontiguousarray(words), np.ascontiguousarray(byte.astype(np.uint8).reshape(n // 512, 16, m))


K, T, S, U, G, H = 512, 2048, 512, 1024, 2048, 512


def setup_inputs():
    n = np.random.standard_normal
    s = mx_kscale(K)[:, None]
    packed_xT = pack_weight(n((K, T)) * s)
    packed_dT = pack_weight(n((K, G)) / s)
    return {
        "x_words": packed_xT[0],
        "x_scales": packed_xT[1],
        "d_words": packed_dT[0],
        "d_scales": packed_dT[1],
        "mem": n((H, U)).astype(np.float32),
        "gs": (np.random.uniform(0.5, 1.5, (K, 1)) * s).astype(np.float32),
        "offs": striped(np.random.permutation(T)[:S]),
        "k1": striped8(np.random.randint(0, G, (8, H))),
        "slot": striped8(np.stack([np.random.permutation(U)[:S] for _ in range(8)])),
        "k2": striped8(np.random.randint(0, G, (8, H))),
    }


def reference(x_words, x_scales, d_words, d_scales, mem, gs, offs, k1, slot, k2):
    d_k2 = unpack_weight(d_words, d_scales)[np.arange(K)[:, None], runs(k2, K)]
    d_k1 = unpack_weight(d_words, d_scales)[np.arange(K)[:, None], runs(k1, K)]
    xq = unpack_weight(x_words, x_scales)[:, unstriped(offs)]
    h = relu(0.0625 * (d_k1.T @ xq))
    pg = f64(mem).copy()
    pg[np.arange(H)[:, None], runs(slot, H)] = h
    z = f64(gs) * pg
    out_0 = 0.0625 * ((d_k2.T @ mxq(z, 0, "e4m3")))
    return (out_0,) + planes(out_0)

@@ -1,0 +1,196 @@
+from contextlib import ExitStack
+
+import concourse.mybir as mybir
+
+F32 = mybir.dt.float32
+BF16 = mybir.dt.bfloat16
+I32 = mybir.dt.int32
+U32 = mybir.dt.uint32
+U16 = mybir.dt.uint16
+U8 = mybir.dt.uint8
+FP8X4 = mybir.dt.float8_e4m3fn_x4
+ACT = mybir.ActivationFunctionType
+MULT = mybir.AluOpType.mult
+
+P = 128
+PACK = 4
+K, T, S, U, G, H = 512, 2048, 512, 1024, 2048, 512
+SIXTEENTH = 0.0625
+CHUNK = 256
+FLOPS = 2 * K * H * S + 2 * K * H * U
+
+
+def tile_picked_pqscat_relu_po_kernel(
+    tc, x_words, x_scales, d_words, d_scales, mem, gs, offs, k1, slot, k2, out_0, out_1, out_2
+):
+    nc = tc.nc
+    with ExitStack() as ctx:
+        lists = ctx.enter_context(tc.tile_pool(name="lists", bufs=1))
+        keep = ctx.enter_context(tc.tile_pool(name="keep", bufs=1))
+        psum = ctx.enter_context(tc.psum_pool(name="psum", bufs=1))
+
+        k1_sb = lists.tile([P, H // 16], U16, name="k1_sb")
+        k2_sb = lists.tile([P, H // 16], U16, name="k2_sb")
+        offs_sb = lists.tile([P, S // 16], U16, name="offs_sb")
+        slot_sb = lists.tile([P, S // 16], U16, name="slot_sb")
+
+        d_scale_table = keep.tile([P, G], U8, name="d_scale_table", align_bytes=64)
+        x_scale_table = keep.tile([P, T], U8, name="x_scale_table", align_bytes=64)
+        w_scales = keep.tile([P, 2 * H], U8, name="w_scales", align_bytes=64)
+        nc.vector.memset(d_scale_table[:].bitcast(I32), 0)
+        nc.vector.memset(x_scale_table[:].bitcast(I32), 0)
+        nc.vector.memset(w_scales[:].bitcast(I32), 0)
+
+        d_word_table = keep.tile([P, G], I32, name="d_word_table", align_bytes=64)
+        x_word_table = keep.tile([P, T], I32, name="x_word_table", tag="x_table", align_bytes=64)
+        gains = keep.tile([P, PACK], F32, name="gains")
+        pages = [keep.tile([P, U], F32, name=f"page{t}", align_bytes=64) for t in range(PACK)]
+        order = (2, 0, 1, 3)
+
+        nc.sync.dma_start(k1_sb[:], k1)
+        nc.scalar.dma_start(d_scale_table[:].bitcast(I32)[0:P:8, :], d_scales[0].bitcast(I32))
+        nc.sync.dma_start(k2_sb[:], k2)
+        nc.sync.dma_start(d_word_table[:], d_words[0].rearrange("p n t -> p (n t)").bitcast(I32))
+        nc.sync.dma_start(offs_sb[:], offs)
+        for q in range(4):
+            nc.scalar.dma_start(
+                x_scale_table[:].bitcast(I32)[32 * q : 32 * q + 4, :], x_scales[0].bitcast(I32)[4 * q : 4 * q + 4, :]
+            )
+        nc.sync.dma_start(x_word_table[:], x_words[0].rearrange("p n t -> p (n t)").bitcast(I32))
+        nc.sync.dma_start(slot_sb[:], slot)
+        nc.sync.dma_start(gains[:], gs.rearrange("(p t) o -> p (t o)", t=PACK))
+        mem_rows = mem.rearrange("(p t) w -> p t w", t=PACK)
+        for t in order:
+            nc.sync.dma_start(pages[t][:], mem_rows[:, t, :])
+
+        picked_scales = keep.tile([P, 2 * H], U8, name="picked_scales", align_bytes=64)
+        dealt_scales = keep.tile([P, 2 * H], U8, name="dealt_scales", align_bytes=64)
+        nc.vector.tensor_copy(picked_scales[:, 0:H], d_scale_table[:].indirect(k1_sb[:]))
+        nc.vector.tensor_copy(picked_scales[:, H : 2 * H], d_scale_table[:].indirect(k2_sb[:]))
+        for u in range(2):
+            nc.vector.tensor_copy(
+                dealt_scales[:, u * H : (u + 1) * H].rearrange("p (t c i) -> p c t i", t=PACK, i=16),
+                picked_scales[:, u * H : (u + 1) * H].rearrange("p (c i t) -> p c t i", t=PACK, i=16),
+            )
+        for q in range(4):
+            nc.scalar.dma_start(
+                w_scales[:].bitcast(I32)[32 * q : 32 * q + 4, :],
+                dealt_scales[:].bitcast(I32)[32 * q : 32 * q + 32 : 8, :],
+            )
+
+        def pick_weight(code_list, name, tag):
+            picked = keep.tile([P, H], I32, name=name + "_picked", tag=tag, align_bytes=64)
+            dealt = keep.tile([P, H], I32, name=name + "_dealt", align_bytes=64)
+            nc.vector.tensor_copy(picked[:].bitcast(U32), d_word_table[:].bitcast(U32).indirect(code_list[:]))
+            nc.vector.tensor_copy(
+                dealt[:].rearrange("p (t c i) -> p c t i", t=PACK, i=4),
+                picked[:].rearrange("p (c i t) -> p c t i", t=PACK, i=4),
+            )
+            return dealt
+
+        x_scales_picked = keep.tile([P, S], U8, name="x_scales_picked", align_bytes=64)
+        nc.vector.tensor_copy(x_scales_picked[:], x_scale_table[:].indirect(offs_sb[:]))
+        w1_words = pick_weight(k1_sb, "w1", "w1_picked")
+        x_words_picked = keep.tile([P, S], I32, name="x_words_picked", align_bytes=64)
+        nc.vector.tensor_copy(x_words_picked[:].bitcast(U32), x_word_table[:].bitcast(U32).indirect(offs_sb[:]))
+        w2_words = pick_weight(k2_sb, "w2", "x_table")
+
+        hidden = {}
+        banks = {}
+
+        def activate(t, tag):
+            hidden[t] = keep.tile([P, S], F32, name=f"hidden{t}", tag=tag, align_bytes=64)
+            nc.scalar.activation(hidden[t][:], banks[t][:], ACT.Relu, scale=SIXTEENTH)
+
+        for t in order:
+            bank = psum.tile([P, S], F32, name=f"bank{t}", tag=f"bank{t}")
+            banks[t] = bank
+            nc.tensor.matmul_mx(
+                bank[:],
+                lhsT=w1_words[:, t * P : (t + 1) * P].bitcast(FP8X4),
+                lhsT_scale=w_scales[:, t * P : (t + 1) * P],
+                rhs=x_words_picked[:].bitcast(FP8X4),
+                rhs_scale=x_scales_picked[:],
+                start=True,
+                stop=True,
+            )
+            if t != order[3]:
+                activate(t, f"hidden{t}")
+
+        z = keep.tile([P, U, PACK], BF16, name="z", align_bytes=64)
+        chunks = [slice(c, c + CHUNK) for c in range(0, U, CHUNK)]
+        for t in order:
+            nc.vector.tensor_copy(pages[t][:].indirect(slot_sb[:]), hidden[t][:])
+            if t == order[2]:
+                for cols in chunks:
+                    nc.scalar.activation(z[:, cols, t], pages[t][:, cols], ACT.Copy, scale=gains[:, t : t + 1])
+            elif t != order[3]:
+                nc.scalar.activation(z[:, :, t], pages[t][:], ACT.Copy, scale=gains[:, t : t + 1])
+            if t == order[0]:
+                activate(order[3], f"hidden{t}")
+
+        last = order[3]
+        z_words = keep.tile([P, U], I32, name="z_words", align_bytes=64)
+        z_scales = keep.tile([P, U], U8, name="z_scales", align_bytes=64)
+        out_words = keep.tile([P, U], I32, name="out_words", align_bytes=64)
+        out_scales = keep.tile([P, U], U8, name="out_scales", align_bytes=64)
+        out_rows = out_0.rearrange("(p t) w -> p t w", t=PACK)
+        out_1_words = out_1[0].rearrange("p n t -> p (n t)").bitcast(I32)
+
+        def weigh_last(cols):
+            nc.vector.tensor_scalar(z[:, cols, last], pages[last][:, cols], gains[:, last : last + 1], None, MULT)
+
+        def quantize_z(cols):
+            nc.vector.quantize_mx(
+                z_words[:, cols].bitcast(FP8X4), z_scales[:, cols], z[:, cols, :].rearrange("p w t -> p (w t)")
+            )
+
+        weigh_last(chunks[0])
+        for c, cols in enumerate(chunks):
+            if c + 1 < len(chunks):
+                weigh_last(chunks[c + 1])
+            quantize_z(cols)
+
+        results = []
+        for c, cols in enumerate(chunks):
+            result = keep.tile([P, PACK, CHUNK], F32, name=f"result{c}", align_bytes=64)
+            results.append(result)
+            for half in range(2):
+                b = (4 + 2 * c + half) % 8
+                bank = psum.tile([P, 2, CHUNK], F32, name=f"acc{c}_{half}", tag=f"bank{b}")
+                for j in range(2):
+                    t = 2 * half + j
+                    nc.tensor.matmul_mx(
+                        bank[:, j, :],
+                        lhsT=w2_words[:, t * P : (t + 1) * P].bitcast(FP8X4),
+                        lhsT_scale=w_scales[:, H + t * P : H + (t + 1) * P],
+                        rhs=z_words[:, cols].bitcast(FP8X4),
+                        rhs_scale=z_scales[:, cols],
+                        start=True,
+                        stop=True,
+                    )
+                pair = slice(2 * half, 2 * half + 2)
+                nc.scalar.activation(result[:, pair, :], bank[:], ACT.Copy, scale=SIXTEENTH)
+                nc.sync.dma_start(out_rows[:, pair, cols], result[:, pair, :])
+
+        rounded = [keep.tile([P, CHUNK, PACK], BF16, name=f"rounded{c}", align_bytes=64) for c in range(len(chunks))]
+
+        def round_result(c):
+            nc.vector.tensor_copy(
+                rounded[c][:].rearrange("p (g i) t -> p g t i", i=4),
+                results[c][:].rearrange("p t (g i) -> p g t i", i=4),
+            )
+
+        round_result(0)
+        for c, cols in enumerate(chunks):
+            if c + 1 < len(chunks):
+                round_result(c + 1)
+            nc.vector.quantize_mx(
+                out_words[:, cols].bitcast(FP8X4), out_scales[:, cols], rounded[c][:].rearrange("p w t -> p (w t)")
+            )
+            nc.sync.dma_start(out_1_words[:, cols], out_words[:, cols])
+        for q in range(4):
+            queue = nc.scalar if q % 2 else nc.sync
+            queue.dma_start(
+                out_2[0].bitcast(I32)[4 * q : 4 * q + 4, :], out_scales[:].bitcast(I32)[32 * q : 32 * q + 4, :]
+            )

@@ -17,6 +17,7 @@ PACK = 4
 K, T, S, U, G, H = 512, 2048, 512, 1024, 2048, 512
 SIXTEENTH = 0.0625
 CHUNK = 256
+SCALAR_COLS = 256
 FLOPS = 2 * K * H * S + 2 * K * H * U
 
 
@@ -34,49 +35,43 @@ def tile_picked_pqscat_relu_po_kernel(
         offs_sb = lists.tile([P, S // 16], U16, name="offs_sb")
         slot_sb = lists.tile([P, S // 16], U16, name="slot_sb")
 
-        d_scale_table = keep.tile([P, G], U8, name="d_scale_table", align_bytes=64)
-        x_scale_table = keep.tile([P, T], U8, name="x_scale_table", align_bytes=64)
-        w_scales = keep.tile([P, 2 * H], U8, name="w_scales", align_bytes=64)
+        d_scale_table = keep.tile([P, G], U8, name="d_scale_table", tag="d_scale_table", align_bytes=64)
+        x_scale_table = keep.tile([P, T], U8, name="x_scale_table", tag="x_scale_table", align_bytes=64)
+        placed_scales = keep.tile([P, 2 * H + S], U8, name="placed_scales", align_bytes=64)
         nc.vector.memset(d_scale_table[:].bitcast(I32), 0)
         nc.vector.memset(x_scale_table[:].bitcast(I32), 0)
-        nc.vector.memset(w_scales[:].bitcast(I32), 0)
+        nc.vector.memset(placed_scales[:].bitcast(I32), 0)
 
-        d_word_table = keep.tile([P, G], I32, name="d_word_table", align_bytes=64)
-        x_word_table = keep.tile([P, T], I32, name="x_word_table", tag="x_table", align_bytes=64)
-        gains = keep.tile([P, PACK], F32, name="gains")
-        pages = [keep.tile([P, U], F32, name=f"page{t}", align_bytes=64) for t in range(PACK)]
+        d_word_table = keep.tile([P, G], I32, name="d_word_table", tag="d_word_table", align_bytes=64)
+        x_word_table = keep.tile([P, T], I32, name="x_word_table", tag="x_word_table", align_bytes=64)
         order = (2, 0, 1, 3)
 
         nc.sync.dma_start(k1_sb[:], k1)
-        nc.scalar.dma_start(d_scale_table[:].bitcast(I32)[0:P:8, :], d_scales[0].bitcast(I32))
-        nc.sync.dma_start(k2_sb[:], k2)
-        nc.sync.dma_start(d_word_table[:], d_words[0].rearrange("p n t -> p (n t)").bitcast(I32))
         nc.sync.dma_start(offs_sb[:], offs)
-        for q in range(4):
-            nc.scalar.dma_start(
-                x_scale_table[:].bitcast(I32)[32 * q : 32 * q + 4, :], x_scales[0].bitcast(I32)[4 * q : 4 * q + 4, :]
-            )
-        nc.sync.dma_start(x_word_table[:], x_words[0].rearrange("p n t -> p (n t)").bitcast(I32))
+        nc.sync.dma_start(k2_sb[:], k2)
         nc.sync.dma_start(slot_sb[:], slot)
-        nc.sync.dma_start(gains[:], gs.rearrange("(p t) o -> p (t o)", t=PACK))
+        nc.sync.dma_start(d_scale_table[:].bitcast(I32)[0:P:8, :], d_scales[0].bitcast(I32))
+        nc.sync.dma_start(x_scale_table[:].bitcast(I32)[0:P:8, :], x_scales[0].bitcast(I32))
+        nc.sync.dma_start(d_word_table[:], d_words[0].rearrange("p n t -> p (n t)").bitcast(I32))
+        nc.sync.dma_start(x_word_table[:], x_words[0].rearrange("p n t -> p (n t)").bitcast(I32))
         mem_rows = mem.rearrange("(p t) w -> p t w", t=PACK)
-        for t in order:
+        pages = {}
+
+        def load_page(t, tag):
+            pages[t] = keep.tile([P, U], F32, name=f"page{t}", tag=tag, align_bytes=64)
             nc.sync.dma_start(pages[t][:], mem_rows[:, t, :])
 
-        picked_scales = keep.tile([P, 2 * H], U8, name="picked_scales", align_bytes=64)
-        dealt_scales = keep.tile([P, 2 * H], U8, name="dealt_scales", align_bytes=64)
-        nc.vector.tensor_copy(picked_scales[:, 0:H], d_scale_table[:].indirect(k1_sb[:]))
-        nc.vector.tensor_copy(picked_scales[:, H : 2 * H], d_scale_table[:].indirect(k2_sb[:]))
-        for u in range(2):
+        def deal_bytes(dealt, picked):
             nc.vector.tensor_copy(
-                dealt_scales[:, u * H : (u + 1) * H].rearrange("p (t c i) -> p c t i", t=PACK, i=16),
-                picked_scales[:, u * H : (u + 1) * H].rearrange("p (c i t) -> p c t i", t=PACK, i=16),
+                dealt.rearrange("p (t c i) -> p c t i", t=PACK, i=16),
+                picked.rearrange("p (c i t) -> p c t i", t=PACK, i=16),
             )
-        for q in range(4):
-            nc.scalar.dma_start(
-                w_scales[:].bitcast(I32)[32 * q : 32 * q + 4, :],
-                dealt_scales[:].bitcast(I32)[32 * q : 32 * q + 32 : 8, :],
-            )
+
+        def place_rows(placed, spread, queues):
+            for q in range(4):
+                queues[q % 2].dma_start(
+                    placed.bitcast(I32)[32 * q : 32 * q + 4, :], spread.bitcast(I32)[32 * q : 32 * q + 32 : 8, :]
+                )
 
         def pick_weight(code_list, name, tag):
             picked = keep.tile([P, H], I32, name=name + "_picked", tag=tag, align_bytes=64)
@@ -88,12 +83,33 @@ def tile_picked_pqscat_relu_po_kernel(
             )
             return dealt
 
-        x_scales_picked = keep.tile([P, S], U8, name="x_scales_picked", align_bytes=64)
-        nc.vector.tensor_copy(x_scales_picked[:], x_scale_table[:].indirect(offs_sb[:]))
-        w1_words = pick_weight(k1_sb, "w1", "w1_picked")
+        picked1 = keep.tile([P, H + S], U8, name="picked1", tag="picked1", align_bytes=64)
+        spread1 = keep.tile([P, H + S], U8, name="spread1", tag="spread1", align_bytes=64)
+        nc.vector.tensor_copy(picked1[:, 0:H], d_scale_table[:].indirect(k1_sb[:]))
+        nc.vector.tensor_copy(picked1[:, H:], x_scale_table[:].indirect(offs_sb[:]))
+        deal_bytes(spread1[:, 0:H], picked1[:, 0:H])
+        nc.vector.tensor_copy(spread1[:, H:].bitcast(I32), picked1[:, H:].bitcast(I32))
+        place_rows(placed_scales[:, 0 : H + S], spread1[:], (nc.sync, nc.scalar))
+        w1_scales = placed_scales[:, 0:H]
+        x_scales_picked = placed_scales[:, H : H + S]
+        w2_scales = placed_scales[:, H + S :]
+
+        w1_words = pick_weight(k1_sb, "w1", "picked1")
+        load_page(order[0], "picked1")
+        load_page(order[1], "spread1")
         x_words_picked = keep.tile([P, S], I32, name="x_words_picked", align_bytes=64)
         nc.vector.tensor_copy(x_words_picked[:].bitcast(U32), x_word_table[:].bitcast(U32).indirect(offs_sb[:]))
-        w2_words = pick_weight(k2_sb, "w2", "x_table")
+
+        picked2 = keep.tile([P, H], U8, name="picked2", tag="x_word_table", align_bytes=64)
+        spread2 = keep.tile([P, H], U8, name="spread2", align_bytes=64)
+        nc.vector.tensor_copy(picked2[:], d_scale_table[:].indirect(k2_sb[:]))
+        deal_bytes(spread2[:], picked2[:])
+        gains = keep.tile([P, PACK], F32, name="gains", tag="d_scale_table", align_bytes=64)
+        nc.sync.dma_start(gains[:], gs.rearrange("(p t) o -> p (t o)", t=PACK))
+        place_rows(w2_scales, spread2[:], (nc.sync, nc.sync))
+        w2_words = pick_weight(k2_sb, "w2", "x_word_table")
+        load_page(order[2], "d_word_table")
+        load_page(order[3], "x_word_table")
 
         hidden = {}
         banks = {}
@@ -108,9 +124,9 @@ def tile_picked_pqscat_relu_po_kernel(
             nc.tensor.matmul_mx(
                 bank[:],
                 lhsT=w1_words[:, t * P : (t + 1) * P].bitcast(FP8X4),
-                lhsT_scale=w_scales[:, t * P : (t + 1) * P],
+                lhsT_scale=w1_scales[:, t * P : (t + 1) * P],
                 rhs=x_words_picked[:].bitcast(FP8X4),
-                rhs_scale=x_scales_picked[:],
+                rhs_scale=x_scales_picked,
                 start=True,
                 stop=True,
             )
@@ -137,6 +153,8 @@ def tile_picked_pqscat_relu_po_kernel(
         out_rows = out_0.rearrange("(p t) w -> p t w", t=PACK)
         out_1_words = out_1[0].rearrange("p n t -> p (n t)").bitcast(I32)
 
+        spans = [slice(0, 128), slice(128, 384), slice(384, 640), slice(640, 896), slice(896, 1024)]
+
         def weigh_last(cols):
             nc.vector.tensor_scalar(z[:, cols, last], pages[last][:, cols], gains[:, last : last + 1], None, MULT)
 
@@ -145,35 +163,43 @@ def tile_picked_pqscat_relu_po_kernel(
                 z_words[:, cols].bitcast(FP8X4), z_scales[:, cols], z[:, cols, :].rearrange("p w t -> p (w t)")
             )
 
-        weigh_last(chunks[0])
-        for c, cols in enumerate(chunks):
-            if c + 1 < len(chunks):
-                weigh_last(chunks[c + 1])
+        by_scalar = slice(U - SCALAR_COLS, U)
+        nc.scalar.activation(z[:, by_scalar, last], pages[last][:, by_scalar], ACT.Copy, scale=gains[:, last : last + 1])
+        weigh_last(spans[0])
+        for c, cols in enumerate(spans):
+            if c + 1 < len(spans) and spans[c + 1].start < by_scalar.start:
+                weigh_last(slice(spans[c + 1].start, min(spans[c + 1].stop, by_scalar.start)))
             quantize_z(cols)
 
         results = []
-        for c, cols in enumerate(chunks):
-            result = keep.tile([P, PACK, CHUNK], F32, name=f"result{c}", align_bytes=64)
+        bank_number = 4
+        for c, cols in enumerate(spans):
+            width = cols.stop - cols.start
+            rows_a_bank = S // width
+            result = keep.tile([P, PACK, width], F32, name=f"result{c}", align_bytes=64)
             results.append(result)
-            for half in range(2):
-                b = (4 + 2 * c + half) % 8
-                bank = psum.tile([P, 2, CHUNK], F32, name=f"acc{c}_{half}", tag=f"bank{b}")
-                for j in range(2):
-                    t = 2 * half + j
+            for t0 in range(0, PACK, rows_a_bank):
+                bank = psum.tile([P, rows_a_bank, width], F32, name=f"acc{c}_{t0}", tag=f"bank{bank_number % 8}")
+                bank_number = bank_number + 1
+                for j in range(rows_a_bank):
+                    t = t0 + j
                     nc.tensor.matmul_mx(
                         bank[:, j, :],
                         lhsT=w2_words[:, t * P : (t + 1) * P].bitcast(FP8X4),
-                        lhsT_scale=w_scales[:, H + t * P : H + (t + 1) * P],
+                        lhsT_scale=w2_scales[:, t * P : (t + 1) * P],
                         rhs=z_words[:, cols].bitcast(FP8X4),
                         rhs_scale=z_scales[:, cols],
                         start=True,
                         stop=True,
                     )
-                pair = slice(2 * half, 2 * half + 2)
-                nc.scalar.activation(result[:, pair, :], bank[:], ACT.Copy, scale=SIXTEENTH)
-                nc.sync.dma_start(out_rows[:, pair, cols], result[:, pair, :])
+                rows = slice(t0, t0 + rows_a_bank)
+                nc.scalar.activation(result[:, rows, :], bank[:], ACT.Copy, scale=SIXTEENTH)
+                nc.sync.dma_start(out_rows[:, rows, cols], result[:, rows, :])
 
-        rounded = [keep.tile([P, CHUNK, PACK], BF16, name=f"rounded{c}", align_bytes=64) for c in range(len(chunks))]
+        rounded = [
+            keep.tile([P, cols.stop - cols.start, PACK], BF16, name=f"rounded{c}", align_bytes=64)
+            for c, cols in enumerate(spans)
+        ]
 
         def round_result(c):
             nc.vector.tensor_copy(
@@ -181,14 +207,17 @@ def tile_picked_pqscat_relu_po_kernel(
                 results[c][:].rearrange("p t (g i) -> p g t i", i=4),
             )
 
+        stored = 0
         round_result(0)
-        for c, cols in enumerate(chunks):
-            if c + 1 < len(chunks):
+        for c, cols in enumerate(spans):
+            if c + 1 < len(spans):
                 round_result(c + 1)
             nc.vector.quantize_mx(
                 out_words[:, cols].bitcast(FP8X4), out_scales[:, cols], rounded[c][:].rearrange("p w t -> p (w t)")
             )
-            nc.sync.dma_start(out_1_words[:, cols], out_words[:, cols])
+            if c > 0:
+                nc.sync.dma_start(out_1_words[:, stored : cols.stop], out_words[:, stored : cols.stop])
+                stored = cols.stop
         for q in range(4):
             queue = nc.scalar if q % 2 else nc.sync
             queue.dma_start(

from contextlib import ExitStack

import concourse.mybir as mybir

F32 = mybir.dt.float32
BF16 = mybir.dt.bfloat16
I32 = mybir.dt.int32
U32 = mybir.dt.uint32
U16 = mybir.dt.uint16
U8 = mybir.dt.uint8
FP8X4 = mybir.dt.float8_e4m3fn_x4
ACT = mybir.ActivationFunctionType
MULT = mybir.AluOpType.mult

P = 128
PACK = 4
K, T, S, U, G, H = 512, 2048, 512, 1024, 2048, 512
SIXTEENTH = 0.0625
CHUNK = 256
SCALAR_COLS = 256
FLOPS = 2 * K * H * S + 2 * K * H * U


def tile_picked_pqscat_relu_po_kernel(
    tc, x_words, x_scales, d_words, d_scales, mem, gs, offs, k1, slot, k2, out_0, out_1, out_2
):
    nc = tc.nc
    with ExitStack() as ctx:
        lists = ctx.enter_context(tc.tile_pool(name="lists", bufs=1))
        keep = ctx.enter_context(tc.tile_pool(name="keep", bufs=1))
        psum = ctx.enter_context(tc.psum_pool(name="psum", bufs=1))

        k1_sb = lists.tile([P, H // 16], U16, name="k1_sb")
        k2_sb = lists.tile([P, H // 16], U16, name="k2_sb")
        offs_sb = lists.tile([P, S // 16], U16, name="offs_sb")
        slot_sb = lists.tile([P, S // 16], U16, name="slot_sb")

        d_scale_table = keep.tile([P, G], U8, name="d_scale_table", tag="d_scale_table", align_bytes=64)
        x_scale_table = keep.tile([P, T], U8, name="x_scale_table", tag="x_scale_table", align_bytes=64)
        placed_scales = keep.tile([P, 2 * H + S], U8, name="placed_scales", align_bytes=64)
        nc.vector.memset(d_scale_table[:].bitcast(I32), 0)
        nc.vector.memset(x_scale_table[:].bitcast(I32), 0)
        nc.vector.memset(placed_scales[:].bitcast(I32), 0)

        d_word_table = keep.tile([P, G], I32, name="d_word_table", tag="d_word_table", align_bytes=64)
        x_word_table = keep.tile([P, T], I32, name="x_word_table", tag="x_word_table", align_bytes=64)
        order = (2, 0, 1, 3)

        nc.sync.dma_start(k1_sb[:], k1)
        nc.sync.dma_start(offs_sb[:], offs)
        nc.sync.dma_start(k2_sb[:], k2)
        nc.sync.dma_start(slot_sb[:], slot)
        nc.sync.dma_start(d_scale_table[:].bitcast(I32)[0:P:8, :], d_scales[0].bitcast(I32))
        nc.sync.dma_start(x_scale_table[:].bitcast(I32)[0:P:8, :], x_scales[0].bitcast(I32))
        nc.sync.dma_start(d_word_table[:], d_words[0].rearrange("p n t -> p (n t)").bitcast(I32))
        nc.sync.dma_start(x_word_table[:], x_words[0].rearrange("p n t -> p (n t)").bitcast(I32))
        mem_rows = mem.rearrange("(p t) w -> p t w", t=PACK)
        pages = {}

        def load_page(t, tag):
            pages[t] = keep.tile([P, U], F32, name=f"page{t}", tag=tag, align_bytes=64)
            nc.sync.dma_start(pages[t][:], mem_rows[:, t, :])

        def deal_bytes(dealt, picked):
            nc.vector.tensor_copy(
                dealt.rearrange("p (t c i) -> p c t i", t=PACK, i=16),
                picked.rearrange("p (c i t) -> p c t i", t=PACK, i=16),
            )

        def place_rows(placed, spread, queues):
            for q in range(4):
                queues[q % 2].dma_start(
                    placed.bitcast(I32)[32 * q : 32 * q + 4, :], spread.bitcast(I32)[32 * q : 32 * q + 32 : 8, :]
                )

        def pick_weight(code_list, name, tag):
            picked = keep.tile([P, H], I32, name=name + "_picked", tag=tag, align_bytes=64)
            dealt = keep.tile([P, H], I32, name=name + "_dealt", align_bytes=64)
            nc.vector.tensor_copy(picked[:].bitcast(U32), d_word_table[:].bitcast(U32).indirect(code_list[:]))
            nc.vector.tensor_copy(
                dealt[:].rearrange("p (t c i) -> p c t i", t=PACK, i=4),
                picked[:].rearrange("p (c i t) -> p c t i", t=PACK, i=4),
            )
            return dealt

        picked1 = keep.tile([P, H + S], U8, name="picked1", tag="picked1", align_bytes=64)
        spread1 = keep.tile([P, H + S], U8, name="spread1", tag="spread1", align_bytes=64)
        nc.vector.tensor_copy(picked1[:, 0:H], d_scale_table[:].indirect(k1_sb[:]))
        nc.vector.tensor_copy(picked1[:, H:], x_scale_table[:].indirect(offs_sb[:]))
        deal_bytes(spread1[:, 0:H], picked1[:, 0:H])
        nc.vector.tensor_copy(spread1[:, H:].bitcast(I32), picked1[:, H:].bitcast(I32))
        place_rows(placed_scales[:, 0 : H + S], spread1[:], (nc.sync, nc.scalar))
        w1_scales = placed_scales[:, 0:H]
        x_scales_picked = placed_scales[:, H : H + S]
        w2_scales = placed_scales[:, H + S :]

        w1_words = pick_weight(k1_sb, "w1", "picked1")
        load_page(order[0], "picked1")
        load_page(order[1], "spread1")
        x_words_picked = keep.tile([P, S], I32, name="x_words_picked", align_bytes=64)
        nc.vector.tensor_copy(x_words_picked[:].bitcast(U32), x_word_table[:].bitcast(U32).indirect(offs_sb[:]))

        picked2 = keep.tile([P, H], U8, name="picked2", tag="x_word_table", align_bytes=64)
        spread2 = keep.tile([P, H], U8, name="spread2", align_bytes=64)
        nc.vector.tensor_copy(picked2[:], d_scale_table[:].indirect(k2_sb[:]))
        deal_bytes(spread2[:], picked2[:])
        gains = keep.tile([P, PACK], F32, name="gains", tag="d_scale_table", align_bytes=64)
        nc.sync.dma_start(gains[:], gs.rearrange("(p t) o -> p (t o)", t=PACK))
        place_rows(w2_scales, spread2[:], (nc.sync, nc.sync))
        w2_words = pick_weight(k2_sb, "w2", "x_word_table")
        load_page(order[2], "d_word_table")
        load_page(order[3], "x_word_table")

        hidden = {}
        banks = {}

        def activate(t, tag):
            hidden[t] = keep.tile([P, S], F32, name=f"hidden{t}", tag=tag, align_bytes=64)
            nc.scalar.activation(hidden[t][:], banks[t][:], ACT.Relu, scale=SIXTEENTH)

        for t in order:
            bank = psum.tile([P, S], F32, name=f"bank{t}", tag=f"bank{t}")
            banks[t] = bank
            nc.tensor.matmul_mx(
                bank[:],
                lhsT=w1_words[:, t * P : (t + 1) * P].bitcast(FP8X4),
                lhsT_scale=w1_scales[:, t * P : (t + 1) * P],
                rhs=x_words_picked[:].bitcast(FP8X4),
                rhs_scale=x_scales_picked,
                start=True,
                stop=True,
            )
            if t != order[3]:
                activate(t, f"hidden{t}")

        z = keep.tile([P, U, PACK], BF16, name="z", align_bytes=64)
        chunks = [slice(c, c + CHUNK) for c in range(0, U, CHUNK)]
        for t in order:
            nc.vector.tensor_copy(pages[t][:].indirect(slot_sb[:]), hidden[t][:])
            if t == order[2]:
                for cols in chunks:
                    nc.scalar.activation(z[:, cols, t], pages[t][:, cols], ACT.Copy, scale=gains[:, t : t + 1])
            elif t != order[3]:
                nc.scalar.activation(z[:, :, t], pages[t][:], ACT.Copy, scale=gains[:, t : t + 1])
            if t == order[0]:
                activate(order[3], f"hidden{t}")

        last = order[3]
        z_words = keep.tile([P, U], I32, name="z_words", align_bytes=64)
        z_scales = keep.tile([P, U], U8, name="z_scales", align_bytes=64)
        out_words = keep.tile([P, U], I32, name="out_words", align_bytes=64)
        out_scales = keep.tile([P, U], U8, name="out_scales", align_bytes=64)
        out_rows = out_0.rearrange("(p t) w -> p t w", t=PACK)
        out_1_words = out_1[0].rearrange("p n t -> p (n t)").bitcast(I32)

        spans = [slice(0, 128), slice(128, 384), slice(384, 640), slice(640, 896), slice(896, 1024)]

        def weigh_last(cols):
            nc.vector.tensor_scalar(z[:, cols, last], pages[last][:, cols], gains[:, last : last + 1], None, MULT)

        def quantize_z(cols):
            nc.vector.quantize_mx(
                z_words[:, cols].bitcast(FP8X4), z_scales[:, cols], z[:, cols, :].rearrange("p w t -> p (w t)")
            )

        by_scalar = slice(U - SCALAR_COLS, U)
        nc.scalar.activation(z[:, by_scalar, last], pages[last][:, by_scalar], ACT.Copy, scale=gains[:, last : last + 1])
        weigh_last(spans[0])
        for c, cols in enumerate(spans):
            if c + 1 < len(spans) and spans[c + 1].start < by_scalar.start:
                weigh_last(slice(spans[c + 1].start, min(spans[c + 1].stop, by_scalar.start)))
            quantize_z(cols)

        results = []
        bank_number = 4
        for c, cols in enumerate(spans):
            width = cols.stop - cols.start
            rows_a_bank = S // width
            result = keep.tile([P, PACK, width], F32, name=f"result{c}", align_bytes=64)
            results.append(result)
            for t0 in range(0, PACK, rows_a_bank):
                bank = psum.tile([P, rows_a_bank, width], F32, name=f"acc{c}_{t0}", tag=f"bank{bank_number % 8}")
                bank_number = bank_number + 1
                for j in range(rows_a_bank):
                    t = t0 + j
                    nc.tensor.matmul_mx(
                        bank[:, j, :],
                        lhsT=w2_words[:, t * P : (t + 1) * P].bitcast(FP8X4),
                        lhsT_scale=w2_scales[:, t * P : (t + 1) * P],
                        rhs=z_words[:, cols].bitcast(FP8X4),
                        rhs_scale=z_scales[:, cols],
                        start=True,
                        stop=True,
                    )
                rows = slice(t0, t0 + rows_a_bank)
                nc.scalar.activation(result[:, rows, :], bank[:], ACT.Copy, scale=SIXTEENTH)
                nc.sync.dma_start(out_rows[:, rows, cols], result[:, rows, :])

        rounded = [
            keep.tile([P, cols.stop - cols.start, PACK], BF16, name=f"rounded{c}", align_bytes=64)
            for c, cols in enumerate(spans)
        ]

        def round_result(c):
            nc.vector.tensor_copy(
                rounded[c][:].rearrange("p (g i) t -> p g t i", i=4),
                results[c][:].rearrange("p t (g i) -> p g t i", i=4),
            )

        stored = 0
        round_result(0)
        for c, cols in enumerate(spans):
            if c + 1 < len(spans):
                round_result(c + 1)
            nc.vector.quantize_mx(
                out_words[:, cols].bitcast(FP8X4), out_scales[:, cols], rounded[c][:].rearrange("p w t -> p (w t)")
            )
            if c > 0:
                nc.sync.dma_start(out_1_words[:, stored : cols.stop], out_words[:, stored : cols.stop])
                stored = cols.stop
        for q in range(4):
            queue = nc.scalar if q % 2 else nc.sync
            queue.dma_start(
                out_2[0].bitcast(I32)[4 * q : 4 * q + 4, :], out_scales[:].bitcast(I32)[32 * q : 32 * q + 4, :]
            )
